import numpy as np, ml_dtypes
CORES = [45,53,77,117,47,55,79,119]
N = 8
import mx_ref
NC, G = 256, 4
M = NC // N
C = np.float32(0.037)
BF = ml_dtypes.bfloat16
def cut(t, i, w=512):
    return t[:, w * i:w * i + w]
def tile(rs):
    return np.stack(rs, axis=2).reshape(128, -1).astype(BF)
def layer(w, X):
    out = []
    for i in range(G):
        for t in range(len(X)):
            p = mx_ref.matmul(mx_ref.quantize(cut(w, len(X) * i + t)), X[t])
            z = p if t == 0 else z + p
        out.append(z)
    return out
def act(Z):
    return [np.maximum(z, 0) * C for z in Z]
def setup_inputs(rng):
    def f(*shape):
        return mx_ref.flush((rng.standard_normal(shape, dtype=np.float32) * np.exp2(rng.integers(-2, 3, shape[:-1] + (1,)))).astype(BF))
    return {"x": f(N, 128, 4 * NC), "w1": f(N, 128, G * 512), "w2": f(N, 128, 512)}
def setup_inputs_blocks(rng):
    d = setup_inputs(rng)
    for k in ("x", "w1", "w2"): d[k] = mx_ref.spread(d[k], rng, 4)
    return d
def setup_inputs_wide(rng):
    d = setup_inputs(rng)
    for k in ("x", "w1", "w2"): d[k] = mx_ref.flush((d[k].astype(np.float32) * np.exp2(rng.integers(-8, 9, (N, 1, 1))).astype(np.float32)).astype(BF))
    return d
def setup_inputs_zeros(rng):
    d = setup_inputs(rng); v = d["x"].reshape(N, 128, -1, 4).copy()
    v[np.broadcast_to((rng.random((N, 1, v.shape[2], 1)) < 0.33), v.shape)] = 0
    d["x"] = v.reshape(d["x"].shape)
    return d
def reference(x, w1, w2):
    h = [tile(act(layer(w1[j], [mx_ref.quantize(x[j])]))) for j in range(N)]
    y = np.zeros((N, 128, NC), np.float32)
    for r in range(N):
        t = np.concatenate([cut(h[j], r, 4 * M) for j in range(N)], axis=1)
        y[r] = mx_ref.matmul(mx_ref.quantize(w2[r]), mx_ref.quantize(t))
    return {"y": y}

from concourse.bass import DstId, RemoteDMATransfer
from concourse.mybir import dt, ActivationFunctionType

N = 8
RUN = 32
NC = N * RUN
HALF = NC // 2
C = 0.037
BANK = 512

FAR_E = 4
FWD_E = 8
PLANE_E = 4
PARTNER_E = 8

SCRATCH = {
    "xs": ("sbuf", [128, 4 * NC], "bfloat16"),
    "w1s": ("sbuf", [128, 4 * 512], "bfloat16"),
    "w2s": ("sbuf", [128, 512], "bfloat16"),
    "xq": ("sbuf", [128, NC], "float8_e4m3fn_x4"), "xp": ("sbuf", [128, NC], "uint8"),
    "w1q": ("sbuf", [128, 512], "float8_e4m3fn_x4"), "w1p": ("sbuf", [128, 512], "uint8"),
    "w2q": ("sbuf", [128, 128], "float8_e4m3fn_x4"), "w2p": ("sbuf", [128, 128], "uint8"),
    "ht": ("sbuf", [128, 4 * NC], "bfloat16"),
    "hq": ("sbuf", [128, NC], "float8_e4m3fn_x4"), "hp": ("sbuf", [128, NC], "uint8"),
    "bnq": ("sbuf", [128, 7 * RUN], "float8_e4m3fn_x4"), "bnp": ("sbuf", [128, 7 * RUN], "uint8"),
    "bfq": ("sbuf", [128, HALF], "float8_e4m3fn_x4"), "bfp": ("sbuf", [128, HALF], "uint8"),
    "fwq": ("sbuf", [128, 2 * RUN], "float8_e4m3fn_x4"), "fwp": ("sbuf", [128, 2 * RUN], "uint8"),
    "ys": ("sbuf", [128, 2, N // 2, RUN], "float32"),
    "ps": ("psum", [128, 7 * BANK], "float32"),
}
SEMAPHORES = ["sx", "sb", "sc", "sd", "se", "vq", "tm", "sa", "hqs", "vo", "an", "af", "fs", "fc", "ls",
              "tyn", "tyf", "cps", "cpv", "st"]


def _bits(mask):
    return [e for e in range(mask.bit_length()) if (mask >> e) & 1]


def _alloc(reqs):
    used, out = 0, [0] * len(reqs)
    for i in sorted(range(len(reqs)), key=lambda k: len(_bits(reqs[k][0]))):
        for e in [e for e in _bits(reqs[i][0]) if not (used >> e) & 1][:reqs[i][1]]:
            out[i] |= 1 << e
        used |= out[i]
    return out


def _routes(cores, topo):
    chips = sorted({topo.chip(c) for c in cores})
    mem = {ch: [c for c in cores if topo.chip(c) == ch] for ch in chips}
    route = {}
    for ch in chips:
        far = [x for x in chips if x != ch and not topo.same_plane(ch, x)]
        dests = [d for x in far for d in mem[x]]
        able = [c for c in range(topo.CHIPS * topo.CORES_PER_CHIP)
                if topo.chip(c) == ch and all(topo.may_write(c, d) for d in dests)]
        idle = [c for c in able if c not in cores]
        home = topo.die(mem[ch][0])
        away = [c for c in idle if topo.die(c) != home]
        near = [c for c in idle if topo.die(c) == home] + [c for c in able if c in cores]
        for i, x in enumerate(far):
            for d, f in zip(mem[x], (away[i], near[i])):
                route[(ch, d)] = f
    return chips, mem, route


def rank_program(g, core, T, topo):
    cores = list(T.cores)
    chips, mem, route = _routes(cores, topo)
    rank = T.rank_of(core)
    me = topo.chip(core)
    S = T.sem
    jobs = [d for (ch, d), f in route.items() if f == core]
    if rank is None and not jobs:
        return
    sent = [0]

    def far_chips(ch):
        return [x for x in chips if x != ch and not topo.same_plane(ch, x)]

    def far_slot(d, src):
        return 2 * RUN * far_chips(topo.chip(d)).index(topo.chip(src)) + RUN * mem[topo.chip(src)].index(src)

    def near_view(d):
        ch = topo.chip(d)
        partner = [c for c in mem[ch] if c != d]
        plane = [c for x in chips if topo.same_plane(ch, x) for c in mem[x]]
        if cores.index(d) + 4 <= N:
            return 0, plane + partner + [d]
        return 3 * RUN, [d] + partner + plane

    def near_slot(d, src):
        base, order = near_view(d)
        return base + RUN * order.index(src)

    def view(name, a, w, codes):
        if codes:
            return T[name + "q"][:, a:a + w].bitcast(dt.uint8)
        return T[name + "p"][:, a:a + w]

    def send(items, codes):
        masks = _alloc([(topo.mask(core, it[0]), it[5]) for it in items])
        trs = []
        for it, m in zip(items, masks):
            rid, pid, _se = topo.addr(it[0])
            trs.append(RemoteDMATransfer(dst_ids=[DstId(rid=rid, pnc=pid)], dma_engine_mask=m, remote_sem=it[4][codes],
                                         src=view("h", it[1], RUN, codes), dst=view(it[2], it[3], RUN, codes)))
            sent[0] += it[5]
        g.remote_dma_fused(trs, local_sem=S.ls)

    def forward():
        d = jobs[0]
        srcs = [c for c in mem[me] if c != core]
        a = RUN * mem[me].index(srcs[0])
        w = RUN * len(srcs)
        rid, pid, _se = topo.addr(d)
        mask = _alloc([(topo.mask(core, d), FWD_E)])[0]
        for codes, sem in ((0, S.fs), (1, S.fc)):
            g.wait_ge(sem, FAR_E * len(srcs))
            g.remote_dma(view("bf", far_slot(d, srcs[0]), w, codes), view("fw", a, w, codes), S.af, S.ls, pid, rid, mask)
            sent[0] += FWD_E

    if rank is None:
        forward()
        g.wait_ge(S.ls, sent[0])
        return

    v, t, s, y = g.vector, g.tensor, g.scalar, g.sync
    Relu, Copy = ActivationFunctionType.Relu, ActivationFunctionType.Copy

    def bank(i, n):
        return T.ps[:, BANK * i:BANK * i + n]

    y.dma_start(T.xs[:], T.x[:]).then_inc(S.sx, 16)
    s.dma_start(T.w1s[:, 0:1024], T.w1[:, 0:1024]).then_inc(S.sb, 16)
    y.dma_start(T.w1s[:, 1024:1536], T.w1[:, 1024:1536]).then_inc(S.sc, 16)
    s.dma_start(T.w1s[:, 1536:2048], T.w1[:, 1536:2048]).then_inc(S.sd, 16)
    y.dma_start(T.w2s[:], T.w2[:]).then_inc(S.se, 16)

    v.wait_ge(S.sx, 16)
    v.quantize_mx(T.xq[:], T.xp[:], T.xs[:]).then_inc(S.vq, 1)
    v.wait_ge(S.sb, 16)
    v.quantize_mx(T.w1q[:, 0:256], T.w1p[:, 0:256], T.w1s[:, 0:1024]).then_inc(S.vq, 1)
    v.wait_ge(S.sc, 16)
    v.quantize_mx(T.w1q[:, 256:384], T.w1p[:, 256:384], T.w1s[:, 1024:1536]).then_inc(S.vq, 1)
    v.wait_ge(S.sd, 16)
    v.quantize_mx(T.w1q[:, 384:512], T.w1p[:, 384:512], T.w1s[:, 1536:2048]).then_inc(S.vq, 1)

    def w1(i):
        return T.w1q[:, 128 * i:128 * i + 128], T.w1p[:, 128 * i:128 * i + 128]

    t.wait_ge(S.vq, 2)
    t.matmul_mx(bank(0, NC), w1(0)[0], w1(0)[1], T.xq[:], T.xp[:], True, True).then_inc(S.tm, 1)
    t.matmul_mx(bank(1, NC), w1(1)[0], w1(1)[1], T.xq[:], T.xp[:], True, True).then_inc(S.tm, 1)
    t.wait_ge(S.vq, 3)
    t.matmul_mx(bank(2, NC), w1(2)[0], w1(2)[1], T.xq[:], T.xp[:], True, True).then_inc(S.tm, 1)
    t.wait_ge(S.vq, 4)
    t.matmul_mx(bank(3, HALF), w1(3)[0], w1(3)[1], T.xq[:, 0:HALF], T.xp[:, 0:HALF], True, True).then_inc(S.tm, 1)
    t.matmul_mx(bank(4, HALF), w1(3)[0], w1(3)[1], T.xq[:, HALF:NC], T.xp[:, HALF:NC], True, True).then_inc(S.tm, 1)

    for b in range(3):
        s.wait_ge(S.tm, b + 1)
        s.activation(T.ht[:, b:4 * NC:4], bank(b, NC), Relu, scale=C).then_inc(S.sa, 1)
    s.wait_ge(S.tm, 4)
    s.activation(T.ht[:, 3:4 * HALF:4], bank(3, HALF), Relu, scale=C).then_inc(S.sa, 1)
    s.wait_ge(S.tm, 5)
    s.activation(T.ht[:, 4 * HALF + 3:4 * NC:4], bank(4, HALF), Relu, scale=C).then_inc(S.sa, 1)

    v.wait_ge(S.sa, 4)
    v.quantize_mx(T.hq[:, 0:HALF], T.hp[:, 0:HALF], T.ht[:, 0:4 * HALF]).then_inc(S.hqs, 1)
    v.wait_ge(S.sa, 5)
    v.quantize_mx(T.hq[:, HALF:NC], T.hp[:, HALF:NC], T.ht[:, 4 * HALF:4 * NC]).then_inc(S.hqs, 1)
    nbase, norder = near_view(core)
    if nbase == 0:
        v.quantize_mx(T.bnq[:, 3 * RUN:7 * RUN], T.bnp[:, 3 * RUN:7 * RUN],
                      T.ht[:, 4 * RUN * rank:4 * RUN * (rank + 4)]).then_inc(S.vo, 1)
    else:
        v.quantize_mx(T.bnq[:, 0:4 * RUN], T.bnp[:, 0:4 * RUN],
                      T.ht[:, 4 * RUN * (rank - 3):4 * RUN * (rank + 1)]).then_inc(S.vo, 1)
    v.wait_ge(S.se, 16)
    v.quantize_mx(T.w2q[:], T.w2p[:], T.w2s[:]).then_inc(S.vo, 1)

    far, near = [], []
    for r, d in enumerate(cores):
        if d == core:
            continue
        if topo.chip(d) == me:
            near.append((d, RUN * r, "bn", near_slot(d, core), (S.an, S.an), PARTNER_E))
        elif topo.same_plane(me, topo.chip(d)):
            near.append((d, RUN * r, "bn", near_slot(d, core), (S.an, S.an), PLANE_E))
        elif route[(me, d)] == core:
            far.append((d, RUN * r, "bf", far_slot(d, core), (S.af, S.af), FAR_E))
        else:
            far.append((route[(me, d)], RUN * r, "fw", RUN * mem[me].index(core), (S.fs, S.fc), FAR_E))
    g.wait_ge(S.hqs, 2)
    send(far, 0)
    send(far, 1)
    send(near, 0)
    send(near, 1)
    if jobs:
        forward()

    n_near = sum(2 * (PARTNER_E if topo.chip(c) == me else PLANE_E) for c in norder if c != core)
    n_far = sum(2 * FWD_E + (2 * FAR_E if route[(x, core)] in cores else 0) for x in far_chips(me))
    t.wait_ge(S.vo, 2)
    t.wait_ge(S.an, n_near)
    t.matmul_mx(bank(5, HALF), T.w2q[:], T.w2p[:], T.bnq[:, nbase:nbase + HALF], T.bnp[:, nbase:nbase + HALF],
                True, True).then_inc(S.tyn, 1)
    t.wait_ge(S.af, n_far)
    t.matmul_mx(bank(6, HALF), T.w2q[:], T.w2p[:], T.bfq[:], T.bfp[:], True, True).then_inc(S.tyf, 1)

    def pieces(order):
        rs, out, p = [cores.index(c) for c in order], [], 0
        while p < len(rs):
            if p + 1 < len(rs) and rs[p + 1] - rs[p] == N // 2:
                out.append((RUN * p, 2 * RUN, T.ys[:, :, rs[p], :]))
                p += 2
            else:
                out.append((RUN * p, RUN, T.ys[:, rs[p] // (N // 2), rs[p] % (N // 2), :]))
                p += 1
        return out

    pn = pieces(norder)
    s.wait_ge(S.tyn, 1)
    for a, w, out in pn:
        s.activation(out, T.ps[:, 5 * BANK + a:5 * BANK + a + w], Copy).then_inc(S.cps, 1)
    pf = pieces([c for x in far_chips(me) for c in mem[x]])
    v.wait_ge(S.tyf, 1)
    for a, w, out in pf:
        v.tensor_copy(out, T.ps[:, 6 * BANK + a:6 * BANK + a + w]).then_inc(S.cpv, 1)

    y.wait_ge(S.cps, len(pn))
    y.wait_ge(S.cpv, len(pf))
    y.dma_start(T.y[:], T.ys[:]).then_inc(S.st, 16)
    y.wait_ge(S.st, 16)
    g.wait_ge(S.ls, sent[0])
